import numpy as np
import ml_dtypes


def mxq(x, axis, fmt="e4m3"):
    dtype, down = {"e4m3": (ml_dtypes.float8_e4m3fn, 7), "e5m2": (ml_dtypes.float8_e5m2, 14)}[fmt]
    v = np.moveaxis(np.asarray(x, np.float32).astype(ml_dtypes.bfloat16).astype(np.float64), axis, -1)
    blocks = v.reshape(v.shape[:-1] + (-1, 32))
    amax = np.abs(blocks).max(-1, keepdims=True)
    byte = np.maximum(np.where(amax > 0, np.frexp(amax)[1] - 1 + 127, 0) - down, 1)
    scale = np.exp2(byte - 127.0)
    codes = (blocks / scale).astype(np.float32).astype(dtype).astype(np.float64)
    return np.moveaxis((codes * scale).reshape(v.shape), -1, axis)


WIDE = False


def mx_kscale(k):
    if not WIDE:
        return np.ones(k)
    levels = np.array([10, -10, 5, -5, 0])
    if k % 512:
        return np.exp2(np.random.permutation(np.resize(levels, k // 32))).repeat(32)
    a = np.empty((k // 512, 16))
    for p in range(k // 512):
        a[p, :8] = np.random.permutation(np.resize(levels, 8))
        for g in range(8):
            far = levels[np.abs(levels - a[p, g]) >= 10]
            a[p, g + 8] = far[np.random.randint(len(far))]
    return np.exp2(a.ravel()).repeat(32)


def f64(x):
    return np.asarray(x).astype(np.float64)


def striped(idx):
    return np.tile(idx.reshape(-1, 16).T, (8, 1)).astype(np.uint16)


def unstriped(offs):
    return offs[:16].T.reshape(-1).astype(np.int64)


def pack_weight(w):
    k, n = w.shape
    w = f64(np.asarray(w, np.float32).astype(ml_dtypes.bfloat16)).reshape(k // 32, 32, n)
    amax = np.abs(w).max(1)
    byte = np.clip(np.where(amax > 0, np.frexp(amax)[1] - 1 + 127 - 7, 1), 1, 254)
    scaled = (w * np.exp2(127.0 - byte)[:, None, :]).reshape(k, n).astype(np.float32)
    words = np.ascontiguousarray(scaled.reshape(k // 512, 128, 4, n).transpose(0, 1, 3, 2)).astype(ml_dtypes.float8_e4m3fn).view(np.uint8)
    return words, np.ascontiguousarray(byte.astype(np.uint8).reshape(k // 512, 16, n))


def unpack_weight(words, scales):
    g, p, n, _ = words.shape
    vals = np.ascontiguousarray(words).view(ml_dtypes.float8_e4m3fn).astype(np.float64) * np.repeat(np.exp2(scales.astype(np.float64) - 127.0), 8, axis=1)[..., None]
    return vals.transpose(0, 1, 3, 2).reshape(g * 512, n)


E2M1 = np.array([0.0, 0.5, 1.0, 1.5, 2.0, 3.0, 4.0, 6.0, -0.0, -0.5, -1.0, -1.5, -2.0, -3.0, -4.0, -6.0])


def pack_fp4(w):
    k, n = w.shape
    w = f64(np.asarray(w, np.float32).astype(ml_dtypes.bfloat16)).reshape(k // 32, 32, n)
    amax = np.abs(w).max(1)
    mant, ex = np.frexp(amax / 6.0)
    byte = np.clip(np.where(amax > 0, np.where(mant > 0.5, ex, ex - 1) + 127, 1), 1, 254)
    scaled = (w * np.exp2(127.0 - byte)[:, None, :]).reshape(k, n).astype(np.float32)
    c = np.ascontiguousarray(scaled.reshape(k // 512, 128, 4, n).transpose(0, 1, 3, 2)).astype(ml_dtypes.float4_e2m1fn).view(np.uint8) & 0xF
    words = (c[..., 0::2] | (c[..., 1::2] << 4)).reshape(k // 512, 128, 2 * n)
    return np.ascontiguousarray(words), np.ascontiguousarray(byte.astype(np.uint8).reshape(k // 512, 16, n))


def unpack_fp4(words, scales):
    g, _, n = scales.shape
    words = np.ascontiguousarray(words).reshape(g, 128, n, 2)
    nib = np.empty((g, 128, n, 4), np.uint8)
    nib[..., 0::2] = words & 0xF
    nib[..., 1::2] = words >> 4
    vals = E2M1[nib] * np.repeat(np.exp2(scales.astype(np.float64) - 127.0), 8, axis=1)[..., None]
    return vals.transpose(0, 1, 3, 2).reshape(g * 512, n)


def sigmoid(v):
    return 1.0 / (1.0 + np.exp(-np.maximum(v, -700.0)))


K, T, S, D, N, H, V, U = 512, 4096, 1024, 4, 128, 512, 256, 512


def setup_inputs():
    n = np.random.standard_normal
    s = mx_kscale(K)[:, None]
    u = mx_kscale(H)
    packed_xT = pack_weight(n((K, T)) * s)
    packed_w1 = pack_fp4(n((K, H)) / np.sqrt(K) / s)
    packed_w2 = pack_fp4(n((K, H)) / np.sqrt(K) / s)
    packed_w3 = pack_fp4(n((H, N)) / np.sqrt(H) / u[:, None])
    return {
        "x_words": packed_xT[0],
        "x_scales": packed_xT[1],
        "w1_words": packed_w1[0],
        "w1_scales": packed_w1[1],
        "w2_words": packed_w2[0],
        "w2_scales": packed_w2[1],
        "loc": (n((H, U))).astype(np.float32),
        "unit": (np.random.uniform(0.6, 1.4, (H, 1)) * u[:, None]).astype(np.float32),
        "w3_words": packed_w3[0],
        "w3_scales": packed_w3[1],
        "offs": striped(np.random.permutation(T)[:S]),
        "gt": striped(np.random.permutation(np.concatenate([np.arange(V), np.random.randint(0, V, U - V)]))),
        "gs": striped(np.random.permutation(np.concatenate([np.arange(V), np.random.randint(0, V, U - V)]))),
    }


def reference(x_words, x_scales, w1_words, w1_scales, w2_words, w2_scales, loc, unit, w3_words, w3_scales, offs, gt, gs):
    xq = unpack_weight(x_words, x_scales)[:, unstriped(offs)]
    yg = unpack_fp4(w2_words, w2_scales).T @ xq
    w_ = np.exp(1.3 * np.tanh(yg))
    y = unpack_fp4(w1_words, w1_scales).T @ xq
    wy = w_ * y
    gist = (wy.reshape(len(wy), -1, D).sum(axis=2)) / (w_.reshape(len(w_), -1, D).sum(axis=2))
    g1 = gist[:, unstriped(gt)]
    g2 = gist[:, unstriped(gs)]
    zd = g1 - (0.6 * g2)
    hid = f64(unit) * (zd * (sigmoid(f64(loc))) + 0.4 * f64(loc))
    return unpack_fp4(w3_words, w3_scales).T @ mxq(hid, 0, "e4m3")

@@ -1,0 +1,241 @@
+from contextlib import ExitStack
+
+import concourse.mybir as mybir
+from concourse.masks import make_identity
+
+K, T, S, D, N, H, V, U = 512, 4096, 1024, 4, 128, 512, 256, 512
+FLOPS = 2 * K * H * S * 2 + 2 * H * N * U
+
+F32 = mybir.dt.float32
+BF16 = mybir.dt.bfloat16
+I32 = mybir.dt.int32
+U32 = mybir.dt.uint32
+U16 = mybir.dt.uint16
+U8 = mybir.dt.uint8
+FP8X4 = mybir.dt.float8_e4m3fn_x4
+FP4X4 = mybir.dt.float4_e2m1fn_x4
+ALU = mybir.AluOpType
+ACT = mybir.ActivationFunctionType
+
+P = 128
+PACK = 4
+BLOCKS = V // P
+RC = 128
+CHUNKS = U // RC
+
+
+def load_scale_rows(queue, plane, rows, quadrants=range(4)):
+    for q in quadrants:
+        queue.dma_start(out=plane[32 * q : 32 * q + 4, :].bitcast(I32), in_=rows[4 * q : 4 * q + 4, :].bitcast(I32))
+
+
+def tile_picked_ygistk_gate_p_kernel(
+    tc, x_words, x_scales, w1_words, w1_scales, w2_words, w2_scales, loc, unit, w3_words, w3_scales, offs, gt, gs, out
+):
+    nc = tc.nc
+    with ExitStack() as ctx:
+        keep = ctx.enter_context(tc.tile_pool(name="keep", bufs=1))
+        ring = ctx.enter_context(tc.tile_pool(name="ring", bufs=3))
+        acc = ctx.enter_context(tc.psum_pool(name="acc", bufs=1))
+        mm = ctx.enter_context(tc.psum_pool(name="mm", bufs=2))
+
+        offs_sb = keep.tile([P, S // 16], U16, name="offs_sb")
+        gt_sb = keep.tile([P, U // 16], U16, name="gt_sb")
+        gs_sb = keep.tile([P, U // 16], U16, name="gs_sb")
+        x_table = keep.tile([P, T], U32, name="x_table", align_bytes=64)
+        xs_table = keep.tile([P, T], U8, name="xs_table", align_bytes=64)
+        w2s_raw = keep.tile([P, H], U8, name="w2s_raw", align_bytes=64)
+        w1s_raw = keep.tile([P, H], U8, name="w1s_raw", align_bytes=64)
+        w2_raw = keep.tile([P, 2 * H], U8, name="w2_raw", align_bytes=64)
+        w1_raw = keep.tile([P, 2 * H], U8, name="w1_raw", tag="late", align_bytes=64)
+
+        nc.vector.memset(xs_table[:].bitcast(I32), 0)
+        nc.gpsimd.memset(w2s_raw[:].bitcast(I32), 0)
+
+        nc.sync.dma_start(out=offs_sb[:], in_=offs)
+        nc.scalar.dma_start(out=w2_raw[:].bitcast(I32), in_=w2_words[0].bitcast(I32))
+        nc.sync.dma_start(out=gt_sb[:], in_=gt)
+        nc.scalar.dma_start(out=w1_raw[:].bitcast(I32), in_=w1_words[0].bitcast(I32))
+        nc.sync.dma_start(out=gs_sb[:], in_=gs)
+        nc.sync.dma_start(out=x_table[:].bitcast(I32), in_=x_words[0].rearrange("p n t -> p (n t)").bitcast(I32))
+        load_scale_rows(nc.scalar, xs_table, x_scales[0])
+        load_scale_rows(nc.gpsimd, w2s_raw, w2_scales[0], range(0, 2))
+        nc.gpsimd.memset(w1s_raw[:].bitcast(I32), 0)
+        load_scale_rows(nc.gpsimd, w2s_raw, w2_scales[0], range(2, 4))
+        load_scale_rows(nc.sync, w1s_raw, w1_scales[0])
+        ident = keep.tile([P, P], F32, name="ident")
+        make_identity(nc, ident[:])
+        unit_sb = keep.tile([P, PACK], F32, name="unit_sb")
+        nc.gpsimd.dma_start(out=unit_sb[:], in_=unit.rearrange("(p t) o -> p (t o)", t=PACK))
+        w3_codes = keep.tile([P, 2 * N], U8, name="w3_codes", align_bytes=64)
+        nc.gpsimd.dma_start(out=w3_codes[:].bitcast(I32), in_=w3_words[0].bitcast(I32))
+        w3_plane = keep.tile([P, N], U8, name="w3_plane", align_bytes=64)
+        nc.gpsimd.memset(w3_plane[:].bitcast(I32), 0)
+
+        w_codes = []
+        w_planes = []
+        for j, raw in enumerate((w2_raw, w1_raw)):
+            codes = keep.tile([P, 2 * H], U8, name="w_codes%d" % j, align_bytes=64)
+            nc.scalar.copy(
+                out=codes[:].bitcast(U16).rearrange("p (t m) -> p t m", t=PACK),
+                in_=raw[:].bitcast(U16).rearrange("p (m t) -> p t m", t=PACK),
+            )
+            w_codes.append(codes)
+        loc_sb = keep.tile([P, PACK, U], F32, name="loc_sb", tag="late", align_bytes=64)
+        nc.sync.dma_start(out=loc_sb[:], in_=loc.rearrange("(p t) r -> p t r", t=PACK))
+        load_scale_rows(nc.sync, w3_plane, w3_scales[0])
+
+        x_codes = []
+        x_planes = []
+
+        def gather_bytes(b):
+            picked = keep.tile([P, P * D], U8, name="xs_picked%d" % b, align_bytes=64)
+            nc.vector.tensor_copy(out=picked[:], in_=xs_table[:].indirect(offs_sb[:, 32 * b : 32 * (b + 1)]))
+            plane = keep.tile([P, P * D], U8, name="x_plane%d" % b, align_bytes=64)
+            nc.vector.tensor_copy(
+                out=plane[:].rearrange("p (d m) -> p d m", d=D), in_=picked[:].rearrange("p (m d) -> p d m", d=D)
+            )
+            x_planes.append(plane)
+
+        def gather_words(b):
+            codes = keep.tile([P, P * D], U32, name="x_codes%d" % b, align_bytes=64)
+            nc.vector.tensor_copy(
+                out=codes[:].rearrange("p (d m) -> p m d", d=D),
+                in_=x_table[:].indirect(offs_sb[:, 32 * b : 32 * (b + 1)]),
+            )
+            x_codes.append(codes)
+
+        def deal_plane(j):
+            plane = keep.tile([P, H], U8, name="w_plane%d" % j, align_bytes=64)
+            nc.vector.tensor_copy(
+                out=plane[:].rearrange("p (t m) -> p t m", t=PACK),
+                in_=(w2s_raw, w1s_raw)[j][:].rearrange("p (m t) -> p t m", t=PACK),
+            )
+            w_planes.append(plane)
+
+        gather_bytes(0)
+        deal_plane(0)
+        gather_words(0)
+        deal_plane(1)
+        gather_bytes(1)
+        gather_words(1)
+
+        den = [acc.tile([P, PACK, P], F32, name="den%d" % b) for b in range(BLOCKS)]
+        num = [acc.tile([P, PACK, P], F32, name="num%d" % b) for b in range(BLOCKS)]
+        units = [(b, d) for b in range(BLOCKS) for d in range(D)]
+        made = {}
+
+        def products(u):
+            b, d = units[u]
+            cols = slice(d * P, (d + 1) * P)
+            banks = []
+            for j in range(2):
+                bank = mm.tile([P, H], F32, name="bank%d" % j)
+                nc.tensor.matmul_mx(
+                    out=bank[:],
+                    lhsT=x_codes[b][:, cols].bitcast(FP8X4),
+                    lhsT_scale=x_planes[b][:, cols],
+                    rhs=w_codes[j][:].bitcast(FP4X4),
+                    rhs_scale=w_planes[j][:],
+                    start=True,
+                    stop=True,
+                )
+                banks.append(bank)
+            th = keep.tile([P, H], F32, name="th%d" % u, tag="th%d" % u)
+            nc.scalar.activation(out=th[:], in_=banks[0][:], func=ACT.Tanh)
+            w = ring.tile([P, H], F32, name="w")
+            nc.scalar.activation(out=w[:], in_=th[:], func=ACT.Exp, scale=1.3)
+            wy = ring.tile([P, H], F32, name="wy")
+            nc.vector.tensor_tensor(out=wy[:], in0=banks[1][:], in1=w[:], op=ALU.mult)
+            made[u] = (w, wy)
+
+        def sums(u):
+            b, d = units[u]
+            for src, dst in zip(made[u], (den, num)):
+                for t in range(PACK):
+                    nc.tensor.matmul(
+                        out=dst[b][:, t, :],
+                        lhsT=src[:, t * P : (t + 1) * P],
+                        rhs=ident[:],
+                        is_transpose=True,
+                        start=(d == 0 and t == 0),
+                        stop=(d == D - 1 and t == PACK - 1),
+                    )
+
+        half_unit = keep.tile([P, PACK], F32, name="half_unit")
+        nc.gpsimd.tensor_scalar(out=half_unit[:], in0=unit_sb[:], scalar1=0.5, scalar2=0.0, op0=ALU.mult, op1=ALU.add)
+        part_unit = keep.tile([P, PACK], F32, name="part_unit")
+        nc.gpsimd.tensor_scalar(out=part_unit[:], in0=unit_sb[:], scalar1=0.4, scalar2=0.0, op0=ALU.mult, op1=ALU.add)
+        gate = []
+        base = []
+
+        def local_terms(c, slot):
+            rs = slice(c * RC, (c + 1) * RC)
+            g = keep.tile([P, PACK, RC], F32, name="gate%d" % c, tag=slot)
+            nc.scalar.activation(out=g[:], in_=loc_sb[:, :, rs], func=ACT.Tanh, scale=0.5)
+            gate.append(g)
+            bs = keep.tile([P, RC, PACK], F32, name="base%d" % c)
+            nc.gpsimd.tensor_tensor(
+                out=bs[:],
+                in0=loc_sb[:, :, rs].rearrange("p t r -> p r t"),
+                in1=part_unit[:].unsqueeze(1).to_broadcast([P, RC, PACK]),
+                op=ALU.mult,
+            )
+            base.append(bs)
+
+        for u in range(len(units)):
+            products(u)
+            if u > 0:
+                sums(u - 1)
+            if 0 <= u - 3 < CHUNKS:
+                local_terms(u - 3, "th%d" % u)
+        sums(len(units) - 1)
+
+        gist = [keep.tile([P, V], F32, name="gist%d" % t) for t in range(PACK)]
+        for b in range(BLOCKS):
+            square = keep.tile([P, PACK, P], F32, name="square%d" % b)
+            nc.scalar.activation(out=square[:], in_=den[b][:], func=ACT.Square)
+            inv = keep.tile([P, PACK, P], F32, name="inv%d" % b, tag="th%d" % (len(units) - 1) if b == 0 else "inv")
+            nc.scalar.activation(out=inv[:], in_=square[:], func=ACT.Abs_reciprocal_sqrt)
+            for t in range(PACK):
+                nc.vector.scalar_tensor_tensor(
+                    out=gist[t][:, b * P : (b + 1) * P],
+                    in0=num[b][:, t, :],
+                    scalar=half_unit[:, t : t + 1],
+                    in1=inv[:, t, :],
+                    op0=ALU.mult,
+                    op1=ALU.mult,
+                )
+
+        for c in range(CHUNKS):
+            ls = slice(c * RC // 16, (c + 1) * RC // 16)
+            own = ring.tile([P, PACK, RC], F32, name="own")
+            other = ring.tile([P, PACK, RC], F32, name="other")
+            for t in range(PACK):
+                if c == 0:
+                    nc.vector.tensor_copy(out=own[:, t, :], in_=gist[t][:].indirect(gt_sb[:, ls]))
+                else:
+                    nc.scalar.activation(out=own[:, t, :], in_=gist[t][:].indirect(gt_sb[:, ls]), func=ACT.Copy)
+                nc.scalar.activation(out=other[:, t, :], in_=gist[t][:].indirect(gs_sb[:, ls]), func=ACT.Copy)
+            zd = ring.tile([P, PACK, RC], F32, name="zd")
+            nc.vector.scalar_tensor_tensor(out=zd[:], in0=other[:], scalar=-0.6, in1=own[:], op0=ALU.mult, op1=ALU.add)
+            gated = ring.tile([P, PACK, RC], F32, name="gated")
+            nc.vector.scalar_tensor_tensor(out=gated[:], in0=gate[c][:], scalar=1.0, in1=zd[:], op0=ALU.add, op1=ALU.mult)
+            hid = ring.tile([P, RC, PACK], BF16, name="hid", align_bytes=64)
+            nc.vector.tensor_tensor(out=hid[:], in0=gated[:].rearrange("p t r -> p r t"), in1=base[c][:], op=ALU.add)
+            h_codes = ring.tile([P, RC], U32, name="h_codes", align_bytes=64)
+            h_plane = ring.tile([P, RC], U8, name="h_plane", align_bytes=64)
+            nc.vector.quantize_mx(out=h_codes[:].bitcast(FP8X4), scales=h_plane[:], in_=hid[:].rearrange("p r t -> p (r t)"))
+            res = mm.tile([P, RC], F32, name="bank0")
+            nc.tensor.matmul_mx(
+                out=res[:],
+                lhsT=w3_codes[:].bitcast(FP4X4),
+                lhsT_scale=w3_plane[:],
+                rhs=h_codes[:].bitcast(FP8X4),
+                rhs_scale=h_plane[:],
+                start=True,
+                stop=True,
+            )
+            res_sb = ring.tile([P, RC], F32, name="res_sb")
+            nc.scalar.copy(out=res_sb[:], in_=res[:])
+            nc.sync.dma_start(out=out[:, c * RC : (c + 1) * RC], in_=res_sb[:])

@@ -1,7 +1,6 @@
 from contextlib import ExitStack
 
 import concourse.mybir as mybir
-from concourse.masks import make_identity
 
 K, T, S, D, N, H, V, U = 512, 4096, 1024, 4, 128, 512, 256, 512
 FLOPS = 2 * K * H * S * 2 + 2 * H * N * U
@@ -20,12 +19,16 @@ ACT = mybir.ActivationFunctionType
 P = 128
 PACK = 4
 BLOCKS = V // P
-RC = 128
-CHUNKS = U // RC
+RC = 256
+HALVES = U // RC
+UNITS = [(t, b) for b in range(BLOCKS) for t in range(PACK)]
+GATE_AFTER = (2, 3, 4, 5)
+ON_VECTOR = {(0, 0, 0), (1, 0, 0)}
+WEAVE_ON_SCALAR = ()
 
 
-def load_scale_rows(queue, plane, rows, quadrants=range(4)):
-    for q in quadrants:
+def load_scale_rows(queue, plane, rows):
+    for q in range(4):
         queue.dma_start(out=plane[32 * q : 32 * q + 4, :].bitcast(I32), in_=rows[4 * q : 4 * q + 4, :].bitcast(I32))
 
 
@@ -35,9 +38,9 @@ def tile_picked_ygistk_gate_p_kernel(
     nc = tc.nc
     with ExitStack() as ctx:
         keep = ctx.enter_context(tc.tile_pool(name="keep", bufs=1))
-        ring = ctx.enter_context(tc.tile_pool(name="ring", bufs=3))
-        acc = ctx.enter_context(tc.psum_pool(name="acc", bufs=1))
-        mm = ctx.enter_context(tc.psum_pool(name="mm", bufs=2))
+        ring = ctx.enter_context(tc.tile_pool(name="ring", bufs=4))
+        gate_banks = ctx.enter_context(tc.psum_pool(name="gate_banks", bufs=4))
+        value_banks = ctx.enter_context(tc.psum_pool(name="value_banks", bufs=4))
 
         offs_sb = keep.tile([P, S // 16], U16, name="offs_sb")
         gt_sb = keep.tile([P, U // 16], U16, name="gt_sb")
@@ -47,186 +50,150 @@ def tile_picked_ygistk_gate_p_kernel(
         w2s_raw = keep.tile([P, H], U8, name="w2s_raw", align_bytes=64)
         w1s_raw = keep.tile([P, H], U8, name="w1s_raw", align_bytes=64)
         w2_raw = keep.tile([P, 2 * H], U8, name="w2_raw", align_bytes=64)
-        w1_raw = keep.tile([P, 2 * H], U8, name="w1_raw", tag="late", align_bytes=64)
+        w1_raw = keep.tile([P, 2 * H], U8, name="w1_raw", align_bytes=64)
+        w3_codes = keep.tile([P, 2 * N], U8, name="w3_codes", align_bytes=64)
+        w3_plane = keep.tile([P, N], U8, name="w3_plane", align_bytes=64)
+        unit_sb = keep.tile([P, PACK], F32, name="unit_sb")
+        loc_sb = keep.tile([P, PACK, U], F32, name="loc_sb")
+        gists = [keep.tile([P, 2 * V], F32, name="gist%d" % t) for t in range(PACK)]
 
-        nc.vector.memset(xs_table[:].bitcast(I32), 0)
-        nc.gpsimd.memset(w2s_raw[:].bitcast(I32), 0)
+        nc.gpsimd.memset(xs_table[:, 0 : T // 2].bitcast(I32), 0)
+        nc.vector.memset(xs_table[:, T // 2 : T].bitcast(I32), 0)
+        for plane in (w2s_raw, w1s_raw, w3_plane):
+            nc.vector.memset(plane[:].bitcast(I32), 0)
 
         nc.sync.dma_start(out=offs_sb[:], in_=offs)
         nc.scalar.dma_start(out=w2_raw[:].bitcast(I32), in_=w2_words[0].bitcast(I32))
-        nc.sync.dma_start(out=gt_sb[:], in_=gt)
-        nc.scalar.dma_start(out=w1_raw[:].bitcast(I32), in_=w1_words[0].bitcast(I32))
-        nc.sync.dma_start(out=gs_sb[:], in_=gs)
+        nc.sync.dma_start(out=w1_raw[:].bitcast(I32), in_=w1_words[0].bitcast(I32))
+        load_scale_rows(nc.sync, xs_table, x_scales[0])
         nc.sync.dma_start(out=x_table[:].bitcast(I32), in_=x_words[0].rearrange("p n t -> p (n t)").bitcast(I32))
-        load_scale_rows(nc.scalar, xs_table, x_scales[0])
-        load_scale_rows(nc.gpsimd, w2s_raw, w2_scales[0], range(0, 2))
-        nc.gpsimd.memset(w1s_raw[:].bitcast(I32), 0)
-        load_scale_rows(nc.gpsimd, w2s_raw, w2_scales[0], range(2, 4))
+        load_scale_rows(nc.gpsimd, w2s_raw, w2_scales[0])
         load_scale_rows(nc.sync, w1s_raw, w1_scales[0])
-        ident = keep.tile([P, P], F32, name="ident")
-        make_identity(nc, ident[:])
-        unit_sb = keep.tile([P, PACK], F32, name="unit_sb")
-        nc.gpsimd.dma_start(out=unit_sb[:], in_=unit.rearrange("(p t) o -> p (t o)", t=PACK))
-        w3_codes = keep.tile([P, 2 * N], U8, name="w3_codes", align_bytes=64)
-        nc.gpsimd.dma_start(out=w3_codes[:].bitcast(I32), in_=w3_words[0].bitcast(I32))
-        w3_plane = keep.tile([P, N], U8, name="w3_plane", align_bytes=64)
-        nc.gpsimd.memset(w3_plane[:].bitcast(I32), 0)
+        nc.sync.dma_start(out=loc_sb[:], in_=loc.rearrange("(p t) r -> p t r", t=PACK))
+        nc.sync.dma_start(out=unit_sb[:], in_=unit.rearrange("(p t) o -> p (t o)", t=PACK))
+        nc.sync.dma_start(out=gt_sb[:], in_=gt)
+        nc.sync.dma_start(out=gs_sb[:], in_=gs)
+        nc.sync.dma_start(out=w3_codes[:].bitcast(I32), in_=w3_words[0].bitcast(I32))
+        load_scale_rows(nc.sync, w3_plane, w3_scales[0])
+        for t in range(PACK):
+            nc.gpsimd.memset(gists[t][:, V : 2 * V], 0.0)
 
         w_codes = []
         w_planes = []
-        for j, raw in enumerate((w2_raw, w1_raw)):
+        for j, (raw, raw_plane) in enumerate(((w2_raw, w2s_raw), (w1_raw, w1s_raw))):
             codes = keep.tile([P, 2 * H], U8, name="w_codes%d" % j, align_bytes=64)
             nc.scalar.copy(
                 out=codes[:].bitcast(U16).rearrange("p (t m) -> p t m", t=PACK),
                 in_=raw[:].bitcast(U16).rearrange("p (m t) -> p t m", t=PACK),
             )
             w_codes.append(codes)
-        loc_sb = keep.tile([P, PACK, U], F32, name="loc_sb", tag="late", align_bytes=64)
-        nc.sync.dma_start(out=loc_sb[:], in_=loc.rearrange("(p t) r -> p t r", t=PACK))
-        load_scale_rows(nc.sync, w3_plane, w3_scales[0])
-
-        x_codes = []
-        x_planes = []
-
-        def gather_bytes(b):
-            picked = keep.tile([P, P * D], U8, name="xs_picked%d" % b, align_bytes=64)
-            nc.vector.tensor_copy(out=picked[:], in_=xs_table[:].indirect(offs_sb[:, 32 * b : 32 * (b + 1)]))
-            plane = keep.tile([P, P * D], U8, name="x_plane%d" % b, align_bytes=64)
-            nc.vector.tensor_copy(
-                out=plane[:].rearrange("p (d m) -> p d m", d=D), in_=picked[:].rearrange("p (m d) -> p d m", d=D)
-            )
-            x_planes.append(plane)
-
-        def gather_words(b):
-            codes = keep.tile([P, P * D], U32, name="x_codes%d" % b, align_bytes=64)
-            nc.vector.tensor_copy(
-                out=codes[:].rearrange("p (d m) -> p m d", d=D),
-                in_=x_table[:].indirect(offs_sb[:, 32 * b : 32 * (b + 1)]),
-            )
-            x_codes.append(codes)
-
-        def deal_plane(j):
             plane = keep.tile([P, H], U8, name="w_plane%d" % j, align_bytes=64)
-            nc.vector.tensor_copy(
+            nc.gpsimd.tensor_copy(
                 out=plane[:].rearrange("p (t m) -> p t m", t=PACK),
-                in_=(w2s_raw, w1s_raw)[j][:].rearrange("p (m t) -> p t m", t=PACK),
+                in_=raw_plane[:].rearrange("p (m t) -> p t m", t=PACK),
             )
             w_planes.append(plane)
+        factors = keep.tile([P, 2, PACK], F32, name="factors")
+        half_unit = factors[:, 0, :]
+        part_unit = factors[:, 1, :]
+        nc.gpsimd.tensor_scalar(out=half_unit, in0=unit_sb[:], scalar1=0.5, scalar2=0.0, op0=ALU.mult, op1=ALU.add)
+        nc.gpsimd.tensor_scalar(out=part_unit, in0=unit_sb[:], scalar1=0.4, scalar2=0.0, op0=ALU.mult, op1=ALU.add)
 
-        gather_bytes(0)
-        deal_plane(0)
-        gather_words(0)
-        deal_plane(1)
-        gather_bytes(1)
-        gather_words(1)
+        x_codes = []
+        x_plane = keep.tile([P, S], U8, name="x_plane", align_bytes=64)
+        nc.vector.tensor_copy(out=x_plane[:], in_=xs_table[:].indirect(offs_sb[:]))
+        for b in range(BLOCKS):
+            entries = offs_sb[:, 32 * b : 32 * (b + 1)]
+            codes = keep.tile([P, P * D], U32, name="x_codes%d" % b, align_bytes=64)
+            nc.vector.tensor_copy(out=codes[:], in_=x_table[:].indirect(entries))
+            x_codes.append(codes)
 
-        den = [acc.tile([P, PACK, P], F32, name="den%d" % b) for b in range(BLOCKS)]
-        num = [acc.tile([P, PACK, P], F32, name="num%d" % b) for b in range(BLOCKS)]
-        units = [(b, d) for b in range(BLOCKS) for d in range(D)]
-        made = {}
+        dens = [keep.tile([P, V], F32, name="den%d" % t) for t in range(PACK)]
+        nums = [keep.tile([P, V], F32, name="num%d" % t) for t in range(PACK)]
+        squares = [keep.tile([P, V], F32, name="square%d" % t) for t in range(PACK)]
+        gates = []
 
         def products(u):
-            b, d = units[u]
-            cols = slice(d * P, (d + 1) * P)
+            t, b = UNITS[u]
             banks = []
-            for j in range(2):
-                bank = mm.tile([P, H], F32, name="bank%d" % j)
+            for j, pool in enumerate((gate_banks, value_banks)):
+                bank = pool.tile([P, P * D], F32, name="bank")
                 nc.tensor.matmul_mx(
                     out=bank[:],
-                    lhsT=x_codes[b][:, cols].bitcast(FP8X4),
-                    lhsT_scale=x_planes[b][:, cols],
-                    rhs=w_codes[j][:].bitcast(FP4X4),
-                    rhs_scale=w_planes[j][:],
+                    lhsT=w_codes[j][:, 2 * t * P : 2 * (t + 1) * P].bitcast(FP4X4),
+                    lhsT_scale=w_planes[j][:, t * P : (t + 1) * P],
+                    rhs=x_codes[b][:].bitcast(FP8X4),
+                    rhs_scale=x_plane[:, b * P * D : (b + 1) * P * D],
                     start=True,
                     stop=True,
                 )
-                banks.append(bank)
-            th = keep.tile([P, H], F32, name="th%d" % u, tag="th%d" % u)
-            nc.scalar.activation(out=th[:], in_=banks[0][:], func=ACT.Tanh)
-            w = ring.tile([P, H], F32, name="w")
+                banks.append(bank[:].rearrange("p (v h e) -> p h v e", h=2, e=2))
+            th = keep.tile([P, 2, P, 2], F32, name="th%d" % u, tag="th%d" % u)
+            nc.scalar.activation(out=th[:], in_=banks[0], func=ACT.Tanh)
+            w = keep.tile([P, 2, P, 2], F32, name="w%d" % u)
             nc.scalar.activation(out=w[:], in_=th[:], func=ACT.Exp, scale=1.3)
-            wy = ring.tile([P, H], F32, name="wy")
-            nc.vector.tensor_tensor(out=wy[:], in0=banks[1][:], in1=w[:], op=ALU.mult)
-            made[u] = (w, wy)
-
-        def sums(u):
-            b, d = units[u]
-            for src, dst in zip(made[u], (den, num)):
-                for t in range(PACK):
-                    nc.tensor.matmul(
-                        out=dst[b][:, t, :],
-                        lhsT=src[:, t * P : (t + 1) * P],
-                        rhs=ident[:],
-                        is_transpose=True,
-                        start=(d == 0 and t == 0),
-                        stop=(d == D - 1 and t == PACK - 1),
-                    )
-
-        half_unit = keep.tile([P, PACK], F32, name="half_unit")
-        nc.gpsimd.tensor_scalar(out=half_unit[:], in0=unit_sb[:], scalar1=0.5, scalar2=0.0, op0=ALU.mult, op1=ALU.add)
-        part_unit = keep.tile([P, PACK], F32, name="part_unit")
-        nc.gpsimd.tensor_scalar(out=part_unit[:], in0=unit_sb[:], scalar1=0.4, scalar2=0.0, op0=ALU.mult, op1=ALU.add)
-        gate = []
-        base = []
-
-        def local_terms(c, slot):
-            rs = slice(c * RC, (c + 1) * RC)
-            g = keep.tile([P, PACK, RC], F32, name="gate%d" % c, tag=slot)
-            nc.scalar.activation(out=g[:], in_=loc_sb[:, :, rs], func=ACT.Tanh, scale=0.5)
-            gate.append(g)
-            bs = keep.tile([P, RC, PACK], F32, name="base%d" % c)
-            nc.gpsimd.tensor_tensor(
-                out=bs[:],
-                in0=loc_sb[:, :, rs].rearrange("p t r -> p r t"),
-                in1=part_unit[:].unsqueeze(1).to_broadcast([P, RC, PACK]),
-                op=ALU.mult,
+            wy = ring.tile([P, 2, P, 2], F32, name="wy")
+            nc.vector.tensor_tensor(out=wy[:], in0=banks[1], in1=w[:], op=ALU.mult)
+            vs = slice(b * P, (b + 1) * P)
+            nc.vector.tensor_reduce(
+                out=nums[t][:, vs], in_=wy[:].rearrange("p h v e -> p v h e"), op=ALU.add, axis=mybir.AxisListType.XY
             )
-            base.append(bs)
+            pair = ring.tile([P, P, 2], F32, name="pair")
+            nc.gpsimd.tensor_tensor(out=pair[:], in0=w[:, 0], in1=w[:, 1], op=ALU.add)
+            nc.gpsimd.tensor_tensor(out=dens[t][:, vs], in0=pair[:, :, 0], in1=pair[:, :, 1], op=ALU.add)
 
-        for u in range(len(units)):
-            products(u)
-            if u > 0:
-                sums(u - 1)
-            if 0 <= u - 3 < CHUNKS:
-                local_terms(u - 3, "th%d" % u)
-        sums(len(units) - 1)
+        def make_gate(u):
+            t = len(gates)
+            g = keep.tile([P, U], F32, name="gate%d" % t, tag="th%d" % u)
+            nc.scalar.activation(out=g[:], in_=loc_sb[:, t, :], func=ACT.Tanh, scale=0.5)
+            gates.append(g)
 
-        gist = [keep.tile([P, V], F32, name="gist%d" % t) for t in range(PACK)]
-        for b in range(BLOCKS):
-            square = keep.tile([P, PACK, P], F32, name="square%d" % b)
-            nc.scalar.activation(out=square[:], in_=den[b][:], func=ACT.Square)
-            inv = keep.tile([P, PACK, P], F32, name="inv%d" % b, tag="th%d" % (len(units) - 1) if b == 0 else "inv")
-            nc.scalar.activation(out=inv[:], in_=square[:], func=ACT.Abs_reciprocal_sqrt)
-            for t in range(PACK):
-                nc.vector.scalar_tensor_tensor(
-                    out=gist[t][:, b * P : (b + 1) * P],
-                    in0=num[b][:, t, :],
-                    scalar=half_unit[:, t : t + 1],
-                    in1=inv[:, t, :],
-                    op0=ALU.mult,
-                    op1=ALU.mult,
-                )
+        def average(t, inv):
+            nc.scalar.activation(out=squares[t][:], in_=dens[t][:], func=ACT.Square)
+            nc.scalar.activation(out=inv, in_=squares[t][:], func=ACT.Abs_reciprocal_sqrt)
+            nc.vector.scalar_tensor_tensor(
+                out=gists[t][:, 0:V], in0=nums[t][:], scalar=half_unit[:, t : t + 1], in1=inv, op0=ALU.mult, op1=ALU.mult
+            )
 
-        for c in range(CHUNKS):
-            ls = slice(c * RC // 16, (c + 1) * RC // 16)
-            own = ring.tile([P, PACK, RC], F32, name="own")
-            other = ring.tile([P, PACK, RC], F32, name="other")
-            for t in range(PACK):
-                if c == 0:
-                    nc.vector.tensor_copy(out=own[:, t, :], in_=gist[t][:].indirect(gt_sb[:, ls]))
+        hid_planes = [keep.tile([P, PACK, RC], BF16, name="hid_planes%d" % h, align_bytes=64) for h in range(HALVES)]
+
+        def read(t, h):
+            rs = slice(h * RC, (h + 1) * RC)
+            ls = slice(h * RC // 16, (h + 1) * RC // 16)
+            fetched = []
+            for i, entries in enumerate((gt_sb, gs_sb)):
+                dst = ring.tile([P, RC], F32, name="fetched%d" % i)
+                if (t, h, i) in ON_VECTOR:
+                    nc.vector.tensor_copy(out=dst[:], in_=gists[t][:].indirect(entries[:, ls]))
                 else:
-                    nc.scalar.activation(out=own[:, t, :], in_=gist[t][:].indirect(gt_sb[:, ls]), func=ACT.Copy)
-                nc.scalar.activation(out=other[:, t, :], in_=gist[t][:].indirect(gs_sb[:, ls]), func=ACT.Copy)
-            zd = ring.tile([P, PACK, RC], F32, name="zd")
-            nc.vector.scalar_tensor_tensor(out=zd[:], in0=other[:], scalar=-0.6, in1=own[:], op0=ALU.mult, op1=ALU.add)
-            gated = ring.tile([P, PACK, RC], F32, name="gated")
-            nc.vector.scalar_tensor_tensor(out=gated[:], in0=gate[c][:], scalar=1.0, in1=zd[:], op0=ALU.add, op1=ALU.mult)
-            hid = ring.tile([P, RC, PACK], BF16, name="hid", align_bytes=64)
-            nc.vector.tensor_tensor(out=hid[:], in0=gated[:].rearrange("p t r -> p r t"), in1=base[c][:], op=ALU.add)
-            h_codes = ring.tile([P, RC], U32, name="h_codes", align_bytes=64)
-            h_plane = ring.tile([P, RC], U8, name="h_plane", align_bytes=64)
+                    nc.scalar.activation(out=dst[:], in_=gists[t][:].indirect(entries[:, ls]), func=ACT.Copy)
+                fetched.append(dst)
+            zd = ring.tile([P, RC], F32, name="zd")
+            nc.vector.scalar_tensor_tensor(
+                out=zd[:], in0=fetched[1][:], scalar=-0.6, in1=fetched[0][:], op0=ALU.mult, op1=ALU.add
+            )
+            gated = ring.tile([P, RC], F32, name="gated")
+            nc.vector.scalar_tensor_tensor(out=gated[:], in0=gates[t][:, rs], scalar=1.0, in1=zd[:], op0=ALU.add, op1=ALU.mult)
+            nc.vector.scalar_tensor_tensor(
+                out=hid_planes[h][:, t, :],
+                in0=loc_sb[:, t, rs],
+                scalar=part_unit[:, t : t + 1],
+                in1=gated[:],
+                op0=ALU.mult,
+                op1=ALU.add,
+            )
+
+        def finish(h):
+            hid = keep.tile([P, RC, PACK], BF16, name="hid%d" % h, align_bytes=64)
+            weave = nc.scalar.copy if h in WEAVE_ON_SCALAR else nc.vector.tensor_copy
+            weave(
+                out=hid[:].rearrange("p (c i) t -> p c t i", i=4),
+                in_=hid_planes[h][:].rearrange("p t (c i) -> p c t i", i=4),
+            )
+            h_codes = keep.tile([P, RC], U32, name="h_codes%d" % h, align_bytes=64)
+            h_plane = keep.tile([P, RC], U8, name="h_plane%d" % h, align_bytes=64)
             nc.vector.quantize_mx(out=h_codes[:].bitcast(FP8X4), scales=h_plane[:], in_=hid[:].rearrange("p r t -> p (r t)"))
-            res = mm.tile([P, RC], F32, name="bank0")
+            res = gate_banks.tile([P, RC], F32, name="bank")
             nc.tensor.matmul_mx(
                 out=res[:],
                 lhsT=w3_codes[:].bitcast(FP4X4),
@@ -236,6 +203,20 @@ def tile_picked_ygistk_gate_p_kernel(
                 start=True,
                 stop=True,
             )
-            res_sb = ring.tile([P, RC], F32, name="res_sb")
+            res_sb = keep.tile([P, RC], F32, name="res_sb%d" % h)
             nc.scalar.copy(out=res_sb[:], in_=res[:])
-            nc.sync.dma_start(out=out[:, c * RC : (c + 1) * RC], in_=res_sb[:])
+            nc.sync.dma_start(out=out[:, h * RC : (h + 1) * RC], in_=res_sb[:])
+
+        for u in range(len(UNITS)):
+            products(u)
+            if u in GATE_AFTER:
+                make_gate(u)
+        invs = keep.tile([P, PACK, V], F32, name="invs", tag="th%d" % (len(UNITS) - 1))
+        for t in range(PACK - 1):
+            average(t, invs[:, t, :])
+        for h in range(HALVES):
+            for t in range(PACK):
+                if (t, h) == (PACK - 2, 0):
+                    average(PACK - 1, invs[:, PACK - 1, :])
+                read(t, h)
+            finish(h)

@@ -1,6 +1,7 @@
 from contextlib import ExitStack
 
 import concourse.mybir as mybir
+from concourse.masks import make_identity
 
 K, T, S, D, N, H, V, U = 512, 4096, 1024, 4, 128, 512, 256, 512
 FLOPS = 2 * K * H * S * 2 + 2 * H * N * U
@@ -19,16 +20,14 @@ ACT = mybir.ActivationFunctionType
 P = 128
 PACK = 4
 BLOCKS = V // P
-RC = 256
-HALVES = U // RC
-UNITS = [(t, b) for b in range(BLOCKS) for t in range(PACK)]
-GATE_AFTER = (2, 3, 4, 5)
-ON_VECTOR = {(0, 0, 0), (1, 0, 0)}
-WEAVE_ON_SCALAR = ()
+WINDOW = 704
+CHUNKS = ((0, 256), (256, 128), (384, 128))
+UNITS = [(2 * g + e, b) for g in range(2) for b in range(BLOCKS) for e in range(2)]
+FIRST_GATE = 3
 
 
-def load_scale_rows(queue, plane, rows):
-    for q in range(4):
+def load_scale_rows(queue, plane, rows, quadrants=range(4)):
+    for q in quadrants:
         queue.dma_start(out=plane[32 * q : 32 * q + 4, :].bitcast(I32), in_=rows[4 * q : 4 * q + 4, :].bitcast(I32))
 
 
@@ -39,8 +38,9 @@ def tile_picked_ygistk_gate_p_kernel(
     with ExitStack() as ctx:
         keep = ctx.enter_context(tc.tile_pool(name="keep", bufs=1))
         ring = ctx.enter_context(tc.tile_pool(name="ring", bufs=4))
-        gate_banks = ctx.enter_context(tc.psum_pool(name="gate_banks", bufs=4))
-        value_banks = ctx.enter_context(tc.psum_pool(name="value_banks", bufs=4))
+        gate_banks = ctx.enter_context(tc.psum_pool(name="gate_banks", bufs=3))
+        value_banks = ctx.enter_context(tc.psum_pool(name="value_banks", bufs=3))
+        den_banks = ctx.enter_context(tc.psum_pool(name="den_banks", bufs=1))
 
         offs_sb = keep.tile([P, S // 16], U16, name="offs_sb")
         gt_sb = keep.tile([P, U // 16], U16, name="gt_sb")
@@ -55,7 +55,7 @@ def tile_picked_ygistk_gate_p_kernel(
         w3_plane = keep.tile([P, N], U8, name="w3_plane", align_bytes=64)
         unit_sb = keep.tile([P, PACK], F32, name="unit_sb")
         loc_sb = keep.tile([P, PACK, U], F32, name="loc_sb")
-        gists = [keep.tile([P, 2 * V], F32, name="gist%d" % t) for t in range(PACK)]
+        gists = [keep.tile([P, WINDOW], F32, name="gist%d" % t) for t in range(PACK)]
 
         nc.gpsimd.memset(xs_table[:, 0 : T // 2].bitcast(I32), 0)
         nc.vector.memset(xs_table[:, T // 2 : T].bitcast(I32), 0)
@@ -67,8 +67,9 @@ def tile_picked_ygistk_gate_p_kernel(
         nc.sync.dma_start(out=w1_raw[:].bitcast(I32), in_=w1_words[0].bitcast(I32))
         load_scale_rows(nc.sync, xs_table, x_scales[0])
         nc.sync.dma_start(out=x_table[:].bitcast(I32), in_=x_words[0].rearrange("p n t -> p (n t)").bitcast(I32))
-        load_scale_rows(nc.gpsimd, w2s_raw, w2_scales[0])
-        load_scale_rows(nc.sync, w1s_raw, w1_scales[0])
+        load_scale_rows(nc.sync, w2s_raw, w2_scales[0])
+        load_scale_rows(nc.gpsimd, w1s_raw, w1_scales[0], range(0, 2))
+        load_scale_rows(nc.sync, w1s_raw, w1_scales[0], range(2, 4))
         nc.sync.dma_start(out=loc_sb[:], in_=loc.rearrange("(p t) r -> p t r", t=PACK))
         nc.sync.dma_start(out=unit_sb[:], in_=unit.rearrange("(p t) o -> p (t o)", t=PACK))
         nc.sync.dma_start(out=gt_sb[:], in_=gt)
@@ -76,7 +77,9 @@ def tile_picked_ygistk_gate_p_kernel(
         nc.sync.dma_start(out=w3_codes[:].bitcast(I32), in_=w3_words[0].bitcast(I32))
         load_scale_rows(nc.sync, w3_plane, w3_scales[0])
         for t in range(PACK):
-            nc.gpsimd.memset(gists[t][:, V : 2 * V], 0.0)
+            nc.gpsimd.memset(gists[t][:, V:WINDOW], 0.0)
+        ident = keep.tile([P, P], F32, name="ident")
+        make_identity(nc, ident[:])
 
         w_codes = []
         w_planes = []
@@ -88,10 +91,8 @@ def tile_picked_ygistk_gate_p_kernel(
             )
             w_codes.append(codes)
             plane = keep.tile([P, H], U8, name="w_plane%d" % j, align_bytes=64)
-            nc.gpsimd.tensor_copy(
-                out=plane[:].rearrange("p (t m) -> p t m", t=PACK),
-                in_=raw_plane[:].rearrange("p (m t) -> p t m", t=PACK),
-            )
+            for t in range(PACK):
+                nc.gpsimd.tensor_copy(out=plane[:, t * P : (t + 1) * P], in_=raw_plane[:, t:H:PACK])
             w_planes.append(plane)
         factors = keep.tile([P, 2, PACK], F32, name="factors")
         half_unit = factors[:, 0, :]
@@ -108,10 +109,12 @@ def tile_picked_ygistk_gate_p_kernel(
             nc.vector.tensor_copy(out=codes[:], in_=x_table[:].indirect(entries))
             x_codes.append(codes)
 
-        dens = [keep.tile([P, V], F32, name="den%d" % t) for t in range(PACK)]
+        dens = [den_banks.tile([P, 2, BLOCKS, P], F32, name="den%d" % g, tag="den%d" % g) for g in range(2)]
+        halves = [keep.tile([P, 2, V], F32, name="halves%d" % t) for t in range(PACK)]
         nums = [keep.tile([P, V], F32, name="num%d" % t) for t in range(PACK)]
-        squares = [keep.tile([P, V], F32, name="square%d" % t) for t in range(PACK)]
+        squares = [keep.tile([P, BLOCKS, P], F32, name="square%d" % t) for t in range(PACK)]
         gates = []
+        weights = []
 
         def products(u):
             t, b = UNITS[u]
@@ -127,73 +130,102 @@ def tile_picked_ygistk_gate_p_kernel(
                     start=True,
                     stop=True,
                 )
-                banks.append(bank[:].rearrange("p (v h e) -> p h v e", h=2, e=2))
-            th = keep.tile([P, 2, P, 2], F32, name="th%d" % u, tag="th%d" % u)
+                banks.append(bank[:].rearrange("p (v d) -> p d v", d=D))
+            th = keep.tile([P, D, P], F32, name="th%d" % u, tag="th%d" % u)
             nc.scalar.activation(out=th[:], in_=banks[0], func=ACT.Tanh)
-            w = keep.tile([P, 2, P, 2], F32, name="w%d" % u)
+            w = keep.tile([P, D, P], F32, name="w%d" % u)
             nc.scalar.activation(out=w[:], in_=th[:], func=ACT.Exp, scale=1.3)
-            wy = ring.tile([P, 2, P, 2], F32, name="wy")
+            weights.append(w)
+            wy = ring.tile([P, D, P], F32, name="wy")
             nc.vector.tensor_tensor(out=wy[:], in0=banks[1], in1=w[:], op=ALU.mult)
-            vs = slice(b * P, (b + 1) * P)
-            nc.vector.tensor_reduce(
-                out=nums[t][:, vs], in_=wy[:].rearrange("p h v e -> p v h e"), op=ALU.add, axis=mybir.AxisListType.XY
-            )
-            pair = ring.tile([P, P, 2], F32, name="pair")
-            nc.gpsimd.tensor_tensor(out=pair[:], in0=w[:, 0], in1=w[:, 1], op=ALU.add)
-            nc.gpsimd.tensor_tensor(out=dens[t][:, vs], in0=pair[:, :, 0], in1=pair[:, :, 1], op=ALU.add)
+            nc.vector.tensor_tensor(out=halves[t][:, :, b * P : (b + 1) * P], in0=wy[:, 0:2], in1=wy[:, 2:4], op=ALU.add)
+            if b == BLOCKS - 1:
+                nc.vector.tensor_tensor(out=nums[t][:], in0=halves[t][:, 0], in1=halves[t][:, 1], op=ALU.add)
+
+        def add_weights(u):
+            t, b = UNITS[u]
+            den = dens[t // 2][:, t % 2]
+            slot = 1 - b if t == 0 else b
+            for d in range(D):
+                nc.tensor.matmul(
+                    out=den[:, slot, :], lhsT=weights[u][:, d, :], rhs=ident[:], is_transpose=True, start=(d == 0), stop=(d == D - 1)
+                )
+            if b == BLOCKS - 1 and t > 0:
+                nc.scalar.activation(out=squares[t][:], in_=den, func=ACT.Square)
 
         def make_gate(u):
-            t = len(gates)
-            g = keep.tile([P, U], F32, name="gate%d" % t, tag="th%d" % u)
-            nc.scalar.activation(out=g[:], in_=loc_sb[:, t, :], func=ACT.Tanh, scale=0.5)
-            gates.append(g)
+            t = u - FIRST_GATE
+            if t % 2 == 0:
+                gates.append(keep.tile([P, 2, U], F32, name="gates%d" % t, tag="th%d" % u))
+            nc.scalar.activation(out=gates[t // 2][:, t % 2, :], in_=loc_sb[:, t, :], func=ACT.Tanh, scale=0.5)
 
-        def average(t, inv):
-            nc.scalar.activation(out=squares[t][:], in_=dens[t][:], func=ACT.Square)
-            nc.scalar.activation(out=inv, in_=squares[t][:], func=ACT.Abs_reciprocal_sqrt)
+        def divide(t, inv, bank):
+            for b in range(BLOCKS):
+                nc.tensor.transpose(bank[:, b * P : (b + 1) * P], inv[:, b, :], ident[:])
             nc.vector.scalar_tensor_tensor(
-                out=gists[t][:, 0:V], in0=nums[t][:], scalar=half_unit[:, t : t + 1], in1=inv, op0=ALU.mult, op1=ALU.mult
+                out=gists[t][:, 0:V], in0=nums[t][:], scalar=half_unit[:, t : t + 1], in1=bank[:], op0=ALU.mult, op1=ALU.mult
             )
 
-        hid_planes = [keep.tile([P, PACK, RC], BF16, name="hid_planes%d" % h, align_bytes=64) for h in range(HALVES)]
+        def average_first():
+            den = dens[0][:, 0]
+            low = keep.tile([P, P], F32, name="low")
+            nc.vector.tensor_copy(out=low[:], in_=den[:, 0, :])
+            both = keep.tile([P, P], F32, name="both")
+            nc.vector.tensor_tensor(out=both[:], in0=den[:, 1, :], in1=low[:], op=ALU.mult)
+            inv_both = keep.tile([P, P], F32, name="inv_both")
+            nc.vector.reciprocal(out=inv_both[:], in_=both[:])
+            inv = keep.tile([P, BLOCKS, P], F32, name="inv_first")
+            nc.vector.tensor_tensor(
+                out=inv[:], in0=den, in1=inv_both[:].unsqueeze(1).to_broadcast([P, BLOCKS, P]), op=ALU.mult
+            )
+            divide(0, inv, den_banks.tile([P, V], F32, name="turned_first", tag="den0"))
 
-        def read(t, h):
-            rs = slice(h * RC, (h + 1) * RC)
-            ls = slice(h * RC // 16, (h + 1) * RC // 16)
-            fetched = []
-            for i, entries in enumerate((gt_sb, gs_sb)):
-                dst = ring.tile([P, RC], F32, name="fetched%d" % i)
-                if (t, h, i) in ON_VECTOR:
-                    nc.vector.tensor_copy(out=dst[:], in_=gists[t][:].indirect(entries[:, ls]))
-                else:
-                    nc.scalar.activation(out=dst[:], in_=gists[t][:].indirect(entries[:, ls]), func=ACT.Copy)
-                fetched.append(dst)
-            zd = ring.tile([P, RC], F32, name="zd")
+        def average_late(t, inv):
+            nc.scalar.activation(out=inv, in_=squares[t][:], func=ACT.Abs_reciprocal_sqrt)
+            divide(t, inv, gate_banks.tile([P, V], F32, name="bank"))
+
+        hid_planes = keep.tile([P, PACK, U], BF16, name="hid_planes", align_bytes=64)
+
+        def read(first, count, start, width, on_vector):
+            rs = slice(start, start + width)
+            ls = slice(start // 16, (start + width) // 16)
+            fetched = [ring.tile([P, count, width], F32, name="fetched%d" % i) for i in range(2)]
+            for e in range(count):
+                for i, entries in enumerate((gt_sb, gs_sb)):
+                    looked_up = gists[first + e][:].indirect(entries[:, ls])
+                    if i < on_vector:
+                        nc.vector.tensor_copy(out=fetched[i][:, e, :], in_=looked_up)
+                    else:
+                        nc.scalar.activation(out=fetched[i][:, e, :], in_=looked_up, func=ACT.Copy)
+            zd = ring.tile([P, count, width], F32, name="zd")
             nc.vector.scalar_tensor_tensor(
                 out=zd[:], in0=fetched[1][:], scalar=-0.6, in1=fetched[0][:], op0=ALU.mult, op1=ALU.add
             )
-            gated = ring.tile([P, RC], F32, name="gated")
-            nc.vector.scalar_tensor_tensor(out=gated[:], in0=gates[t][:, rs], scalar=1.0, in1=zd[:], op0=ALU.add, op1=ALU.mult)
-            nc.vector.scalar_tensor_tensor(
-                out=hid_planes[h][:, t, :],
-                in0=loc_sb[:, t, rs],
-                scalar=part_unit[:, t : t + 1],
-                in1=gated[:],
-                op0=ALU.mult,
-                op1=ALU.add,
-            )
+            gated = ring.tile([P, count, width], F32, name="gated")
+            gate = gates[first // 2][:, first % 2 : first % 2 + count, rs]
+            nc.vector.scalar_tensor_tensor(out=gated[:], in0=gate, scalar=1.0, in1=zd[:], op0=ALU.add, op1=ALU.mult)
+            for e in range(count):
+                t = first + e
+                nc.vector.scalar_tensor_tensor(
+                    out=hid_planes[:, t, rs],
+                    in0=loc_sb[:, t, rs],
+                    scalar=part_unit[:, t : t + 1],
+                    in1=gated[:, e, :],
+                    op0=ALU.mult,
+                    op1=ALU.add,
+                )
 
-        def finish(h):
-            hid = keep.tile([P, RC, PACK], BF16, name="hid%d" % h, align_bytes=64)
-            weave = nc.scalar.copy if h in WEAVE_ON_SCALAR else nc.vector.tensor_copy
-            weave(
+        def finish(start, width):
+            rs = slice(start, start + width)
+            hid = keep.tile([P, width, PACK], BF16, name="hid%d" % start, align_bytes=64)
+            nc.vector.tensor_copy(
                 out=hid[:].rearrange("p (c i) t -> p c t i", i=4),
-                in_=hid_planes[h][:].rearrange("p t (c i) -> p c t i", i=4),
+                in_=hid_planes[:, :, rs].rearrange("p t (c i) -> p c t i", i=4),
             )
-            h_codes = keep.tile([P, RC], U32, name="h_codes%d" % h, align_bytes=64)
-            h_plane = keep.tile([P, RC], U8, name="h_plane%d" % h, align_bytes=64)
+            h_codes = keep.tile([P, width], U32, name="h_codes%d" % start, align_bytes=64)
+            h_plane = keep.tile([P, width], U8, name="h_plane%d" % start, align_bytes=64)
             nc.vector.quantize_mx(out=h_codes[:].bitcast(FP8X4), scales=h_plane[:], in_=hid[:].rearrange("p r t -> p (r t)"))
-            res = gate_banks.tile([P, RC], F32, name="bank")
+            res = value_banks.tile([P, width], F32, name="bank")
             nc.tensor.matmul_mx(
                 out=res[:],
                 lhsT=w3_codes[:].bitcast(FP4X4),
@@ -203,20 +235,25 @@ def tile_picked_ygistk_gate_p_kernel(
                 start=True,
                 stop=True,
             )
-            res_sb = keep.tile([P, RC], F32, name="res_sb%d" % h)
+            res_sb = keep.tile([P, width], F32, name="res_sb%d" % start)
             nc.scalar.copy(out=res_sb[:], in_=res[:])
-            nc.sync.dma_start(out=out[:, h * RC : (h + 1) * RC], in_=res_sb[:])
+            nc.sync.dma_start(out=out[:, rs], in_=res_sb[:])
 
+        last = len(UNITS) - 1
         for u in range(len(UNITS)):
             products(u)
-            if u in GATE_AFTER:
+            if FIRST_GATE <= u < FIRST_GATE + PACK:
                 make_gate(u)
-        invs = keep.tile([P, PACK, V], F32, name="invs", tag="th%d" % (len(UNITS) - 1))
-        for t in range(PACK - 1):
-            average(t, invs[:, t, :])
-        for h in range(HALVES):
-            for t in range(PACK):
-                if (t, h) == (PACK - 2, 0):
-                    average(PACK - 1, invs[:, PACK - 1, :])
-                read(t, h)
-            finish(h)
+            if u > 0:
+                add_weights(u - 1)
+        add_weights(last)
+        average_first()
+        invs = keep.tile([P, PACK - 1, BLOCKS, P], F32, name="invs", tag="th%d" % last)
+        for t in range(1, PACK):
+            average_late(t, invs[:, t - 1])
+        read(0, 1, 0, U // 2, 2)
+        read(0, 1, U // 2, U // 2, 1)
+        read(1, 1, 0, U, 1)
+        for start, width in CHUNKS:
+            read(2, 2, start, width, 0)
+            finish(start, width)

@@ -64,15 +64,15 @@ def tile_picked_ygistk_gate_p_kernel(
 
         nc.sync.dma_start(out=offs_sb[:], in_=offs)
         nc.scalar.dma_start(out=w2_raw[:].bitcast(I32), in_=w2_words[0].bitcast(I32))
-        nc.sync.dma_start(out=w1_raw[:].bitcast(I32), in_=w1_words[0].bitcast(I32))
+        nc.sync.dma_start(out=gt_sb[:], in_=gt)
         load_scale_rows(nc.sync, xs_table, x_scales[0])
         nc.sync.dma_start(out=x_table[:].bitcast(I32), in_=x_words[0].rearrange("p n t -> p (n t)").bitcast(I32))
         load_scale_rows(nc.sync, w2s_raw, w2_scales[0])
+        nc.sync.dma_start(out=w1_raw[:].bitcast(I32), in_=w1_words[0].bitcast(I32))
         load_scale_rows(nc.gpsimd, w1s_raw, w1_scales[0], range(0, 2))
         load_scale_rows(nc.sync, w1s_raw, w1_scales[0], range(2, 4))
         nc.sync.dma_start(out=loc_sb[:], in_=loc.rearrange("(p t) r -> p t r", t=PACK))
         nc.sync.dma_start(out=unit_sb[:], in_=unit.rearrange("(p t) o -> p (t o)", t=PACK))
-        nc.sync.dma_start(out=gt_sb[:], in_=gt)
         nc.sync.dma_start(out=gs_sb[:], in_=gs)
         nc.sync.dma_start(out=w3_codes[:].bitcast(I32), in_=w3_words[0].bitcast(I32))
         load_scale_rows(nc.sync, w3_plane, w3_scales[0])
@@ -189,18 +189,23 @@ def tile_picked_ygistk_gate_p_kernel(
         def read(first, count, start, width, on_vector):
             rs = slice(start, start + width)
             ls = slice(start // 16, (start + width) // 16)
-            fetched = [ring.tile([P, count, width], F32, name="fetched%d" % i) for i in range(2)]
-            for e in range(count):
-                for i, entries in enumerate((gt_sb, gs_sb)):
-                    looked_up = gists[first + e][:].indirect(entries[:, ls])
-                    if i < on_vector:
-                        nc.vector.tensor_copy(out=fetched[i][:, e, :], in_=looked_up)
-                    else:
-                        nc.scalar.activation(out=fetched[i][:, e, :], in_=looked_up, func=ACT.Copy)
             zd = ring.tile([P, count, width], F32, name="zd")
-            nc.vector.scalar_tensor_tensor(
-                out=zd[:], in0=fetched[1][:], scalar=-0.6, in1=fetched[0][:], op0=ALU.mult, op1=ALU.add
-            )
+            if on_vector == 1:
+                other = ring.tile([P, width], F32, name="other")
+                nc.scalar.activation(out=other[:], in_=gists[first][:].indirect(gs_sb[:, ls]), func=ACT.Copy, scale=-0.6)
+                nc.vector.tensor_tensor(out=zd[:, 0, :], in0=gists[first][:].indirect(gt_sb[:, ls]), in1=other[:], op=ALU.add)
+            else:
+                fetched = [ring.tile([P, count, width], F32, name="fetched%d" % i) for i in range(2)]
+                for e in range(count):
+                    for i, entries in enumerate((gt_sb, gs_sb)):
+                        looked_up = gists[first + e][:].indirect(entries[:, ls])
+                        if on_vector:
+                            nc.vector.tensor_copy(out=fetched[i][:, e, :], in_=looked_up)
+                        else:
+                            nc.scalar.activation(out=fetched[i][:, e, :], in_=looked_up, func=ACT.Copy)
+                nc.vector.scalar_tensor_tensor(
+                    out=zd[:], in0=fetched[1][:], scalar=-0.6, in1=fetched[0][:], op0=ALU.mult, op1=ALU.add
+                )
             gated = ring.tile([P, count, width], F32, name="gated")
             gate = gates[first // 2][:, first % 2 : first % 2 + count, rs]
             nc.vector.scalar_tensor_tensor(out=gated[:], in0=gate, scalar=1.0, in1=zd[:], op0=ALU.add, op1=ALU.mult)
@@ -218,7 +223,8 @@ def tile_picked_ygistk_gate_p_kernel(
         def finish(start, width):
             rs = slice(start, start + width)
             hid = keep.tile([P, width, PACK], BF16, name="hid%d" % start, align_bytes=64)
-            nc.vector.tensor_copy(
+            weave = nc.vector.tensor_copy if start + width == U else nc.scalar.copy
+            weave(
                 out=hid[:].rearrange("p (c i) t -> p c t i", i=4),
                 in_=hid_planes[:, :, rs].rearrange("p t (c i) -> p c t i", i=4),
             )

from contextlib import ExitStack

import concourse.mybir as mybir
from concourse.masks import make_identity

K, T, S, D, N, H, V, U = 512, 4096, 1024, 4, 128, 512, 256, 512
FLOPS = 2 * K * H * S * 2 + 2 * H * N * U

F32 = mybir.dt.float32
BF16 = mybir.dt.bfloat16
I32 = mybir.dt.int32
U32 = mybir.dt.uint32
U16 = mybir.dt.uint16
U8 = mybir.dt.uint8
FP8X4 = mybir.dt.float8_e4m3fn_x4
FP4X4 = mybir.dt.float4_e2m1fn_x4
ALU = mybir.AluOpType
ACT = mybir.ActivationFunctionType

P = 128
PACK = 4
BLOCKS = V // P
WINDOW = 704
CHUNKS = ((0, 256), (256, 128), (384, 128))
UNITS = [(2 * g + e, b) for g in range(2) for b in range(BLOCKS) for e in range(2)]
FIRST_GATE = 3


def load_scale_rows(queue, plane, rows, quadrants=range(4)):
    for q in quadrants:
        queue.dma_start(out=plane[32 * q : 32 * q + 4, :].bitcast(I32), in_=rows[4 * q : 4 * q + 4, :].bitcast(I32))


def tile_picked_ygistk_gate_p_kernel(
    tc, x_words, x_scales, w1_words, w1_scales, w2_words, w2_scales, loc, unit, w3_words, w3_scales, offs, gt, gs, out
):
    nc = tc.nc
    with ExitStack() as ctx:
        keep = ctx.enter_context(tc.tile_pool(name="keep", bufs=1))
        ring = ctx.enter_context(tc.tile_pool(name="ring", bufs=4))
        gate_banks = ctx.enter_context(tc.psum_pool(name="gate_banks", bufs=3))
        value_banks = ctx.enter_context(tc.psum_pool(name="value_banks", bufs=3))
        den_banks = ctx.enter_context(tc.psum_pool(name="den_banks", bufs=1))

        offs_sb = keep.tile([P, S // 16], U16, name="offs_sb")
        gt_sb = keep.tile([P, U // 16], U16, name="gt_sb")
        gs_sb = keep.tile([P, U // 16], U16, name="gs_sb")
        x_table = keep.tile([P, T], U32, name="x_table", align_bytes=64)
        xs_table = keep.tile([P, T], U8, name="xs_table", align_bytes=64)
        w2s_raw = keep.tile([P, H], U8, name="w2s_raw", align_bytes=64)
        w1s_raw = keep.tile([P, H], U8, name="w1s_raw", align_bytes=64)
        w2_raw = keep.tile([P, 2 * H], U8, name="w2_raw", align_bytes=64)
        w1_raw = keep.tile([P, 2 * H], U8, name="w1_raw", align_bytes=64)
        w3_codes = keep.tile([P, 2 * N], U8, name="w3_codes", align_bytes=64)
        w3_plane = keep.tile([P, N], U8, name="w3_plane", align_bytes=64)
        unit_sb = keep.tile([P, PACK], F32, name="unit_sb")
        loc_sb = keep.tile([P, PACK, U], F32, name="loc_sb")
        gists = [keep.tile([P, WINDOW], F32, name="gist%d" % t) for t in range(PACK)]

        nc.gpsimd.memset(xs_table[:, 0 : T // 2].bitcast(I32), 0)
        nc.vector.memset(xs_table[:, T // 2 : T].bitcast(I32), 0)
        for plane in (w2s_raw, w1s_raw, w3_plane):
            nc.vector.memset(plane[:].bitcast(I32), 0)

        nc.sync.dma_start(out=offs_sb[:], in_=offs)
        nc.scalar.dma_start(out=w2_raw[:].bitcast(I32), in_=w2_words[0].bitcast(I32))
        nc.sync.dma_start(out=gt_sb[:], in_=gt)
        load_scale_rows(nc.sync, xs_table, x_scales[0])
        nc.sync.dma_start(out=x_table[:].bitcast(I32), in_=x_words[0].rearrange("p n t -> p (n t)").bitcast(I32))
        load_scale_rows(nc.sync, w2s_raw, w2_scales[0])
        nc.sync.dma_start(out=w1_raw[:].bitcast(I32), in_=w1_words[0].bitcast(I32))
        load_scale_rows(nc.gpsimd, w1s_raw, w1_scales[0], range(0, 2))
        load_scale_rows(nc.sync, w1s_raw, w1_scales[0], range(2, 4))
        nc.sync.dma_start(out=loc_sb[:], in_=loc.rearrange("(p t) r -> p t r", t=PACK))
        nc.sync.dma_start(out=unit_sb[:], in_=unit.rearrange("(p t) o -> p (t o)", t=PACK))
        nc.sync.dma_start(out=gs_sb[:], in_=gs)
        nc.sync.dma_start(out=w3_codes[:].bitcast(I32), in_=w3_words[0].bitcast(I32))
        load_scale_rows(nc.sync, w3_plane, w3_scales[0])
        for t in range(PACK):
            nc.gpsimd.memset(gists[t][:, V:WINDOW], 0.0)
        ident = keep.tile([P, P], F32, name="ident")
        make_identity(nc, ident[:])

        w_codes = []
        w_planes = []
        for j, (raw, raw_plane) in enumerate(((w2_raw, w2s_raw), (w1_raw, w1s_raw))):
            codes = keep.tile([P, 2 * H], U8, name="w_codes%d" % j, align_bytes=64)
            nc.scalar.copy(
                out=codes[:].bitcast(U16).rearrange("p (t m) -> p t m", t=PACK),
                in_=raw[:].bitcast(U16).rearrange("p (m t) -> p t m", t=PACK),
            )
            w_codes.append(codes)
            plane = keep.tile([P, H], U8, name="w_plane%d" % j, align_bytes=64)
            for t in range(PACK):
                nc.gpsimd.tensor_copy(out=plane[:, t * P : (t + 1) * P], in_=raw_plane[:, t:H:PACK])
            w_planes.append(plane)
        factors = keep.tile([P, 2, PACK], F32, name="factors")
        half_unit = factors[:, 0, :]
        part_unit = factors[:, 1, :]
        nc.gpsimd.tensor_scalar(out=half_unit, in0=unit_sb[:], scalar1=0.5, scalar2=0.0, op0=ALU.mult, op1=ALU.add)
        nc.gpsimd.tensor_scalar(out=part_unit, in0=unit_sb[:], scalar1=0.4, scalar2=0.0, op0=ALU.mult, op1=ALU.add)

        x_codes = []
        x_plane = keep.tile([P, S], U8, name="x_plane", align_bytes=64)
        nc.vector.tensor_copy(out=x_plane[:], in_=xs_table[:].indirect(offs_sb[:]))
        for b in range(BLOCKS):
            entries = offs_sb[:, 32 * b : 32 * (b + 1)]
            codes = keep.tile([P, P * D], U32, name="x_codes%d" % b, align_bytes=64)
            nc.vector.tensor_copy(out=codes[:], in_=x_table[:].indirect(entries))
            x_codes.append(codes)

        dens = [den_banks.tile([P, 2, BLOCKS, P], F32, name="den%d" % g, tag="den%d" % g) for g in range(2)]
        halves = [keep.tile([P, 2, V], F32, name="halves%d" % t) for t in range(PACK)]
        nums = [keep.tile([P, V], F32, name="num%d" % t) for t in range(PACK)]
        squares = [keep.tile([P, BLOCKS, P], F32, name="square%d" % t) for t in range(PACK)]
        gates = []
        weights = []

        def products(u):
            t, b = UNITS[u]
            banks = []
            for j, pool in enumerate((gate_banks, value_banks)):
                bank = pool.tile([P, P * D], F32, name="bank")
                nc.tensor.matmul_mx(
                    out=bank[:],
                    lhsT=w_codes[j][:, 2 * t * P : 2 * (t + 1) * P].bitcast(FP4X4),
                    lhsT_scale=w_planes[j][:, t * P : (t + 1) * P],
                    rhs=x_codes[b][:].bitcast(FP8X4),
                    rhs_scale=x_plane[:, b * P * D : (b + 1) * P * D],
                    start=True,
                    stop=True,
                )
                banks.append(bank[:].rearrange("p (v d) -> p d v", d=D))
            th = keep.tile([P, D, P], F32, name="th%d" % u, tag="th%d" % u)
            nc.scalar.activation(out=th[:], in_=banks[0], func=ACT.Tanh)
            w = keep.tile([P, D, P], F32, name="w%d" % u)
            nc.scalar.activation(out=w[:], in_=th[:], func=ACT.Exp, scale=1.3)
            weights.append(w)
            wy = ring.tile([P, D, P], F32, name="wy")
            nc.vector.tensor_tensor(out=wy[:], in0=banks[1], in1=w[:], op=ALU.mult)
            nc.vector.tensor_tensor(out=halves[t][:, :, b * P : (b + 1) * P], in0=wy[:, 0:2], in1=wy[:, 2:4], op=ALU.add)
            if b == BLOCKS - 1:
                nc.vector.tensor_tensor(out=nums[t][:], in0=halves[t][:, 0], in1=halves[t][:, 1], op=ALU.add)

        def add_weights(u):
            t, b = UNITS[u]
            den = dens[t // 2][:, t % 2]
            slot = 1 - b if t == 0 else b
            for d in range(D):
                nc.tensor.matmul(
                    out=den[:, slot, :], lhsT=weights[u][:, d, :], rhs=ident[:], is_transpose=True, start=(d == 0), stop=(d == D - 1)
                )
            if b == BLOCKS - 1 and t > 0:
                nc.scalar.activation(out=squares[t][:], in_=den, func=ACT.Square)

        def make_gate(u):
            t = u - FIRST_GATE
            if t % 2 == 0:
                gates.append(keep.tile([P, 2, U], F32, name="gates%d" % t, tag="th%d" % u))
            nc.scalar.activation(out=gates[t // 2][:, t % 2, :], in_=loc_sb[:, t, :], func=ACT.Tanh, scale=0.5)

        def divide(t, inv, bank):
            for b in range(BLOCKS):
                nc.tensor.transpose(bank[:, b * P : (b + 1) * P], inv[:, b, :], ident[:])
            nc.vector.scalar_tensor_tensor(
                out=gists[t][:, 0:V], in0=nums[t][:], scalar=half_unit[:, t : t + 1], in1=bank[:], op0=ALU.mult, op1=ALU.mult
            )

        def average_first():
            den = dens[0][:, 0]
            low = keep.tile([P, P], F32, name="low")
            nc.vector.tensor_copy(out=low[:], in_=den[:, 0, :])
            both = keep.tile([P, P], F32, name="both")
            nc.vector.tensor_tensor(out=both[:], in0=den[:, 1, :], in1=low[:], op=ALU.mult)
            inv_both = keep.tile([P, P], F32, name="inv_both")
            nc.vector.reciprocal(out=inv_both[:], in_=both[:])
            inv = keep.tile([P, BLOCKS, P], F32, name="inv_first")
            nc.vector.tensor_tensor(
                out=inv[:], in0=den, in1=inv_both[:].unsqueeze(1).to_broadcast([P, BLOCKS, P]), op=ALU.mult
            )
            divide(0, inv, den_banks.tile([P, V], F32, name="turned_first", tag="den0"))

        def average_late(t, inv):
            nc.scalar.activation(out=inv, in_=squares[t][:], func=ACT.Abs_reciprocal_sqrt)
            divide(t, inv, gate_banks.tile([P, V], F32, name="bank"))

        hid_planes = keep.tile([P, PACK, U], BF16, name="hid_planes", align_bytes=64)

        def read(first, count, start, width, on_vector):
            rs = slice(start, start + width)
            ls = slice(start // 16, (start + width) // 16)
            zd = ring.tile([P, count, width], F32, name="zd")
            if on_vector == 1:
                other = ring.tile([P, width], F32, name="other")
                nc.scalar.activation(out=other[:], in_=gists[first][:].indirect(gs_sb[:, ls]), func=ACT.Copy, scale=-0.6)
                nc.vector.tensor_tensor(out=zd[:, 0, :], in0=gists[first][:].indirect(gt_sb[:, ls]), in1=other[:], op=ALU.add)
            else:
                fetched = [ring.tile([P, count, width], F32, name="fetched%d" % i) for i in range(2)]
                for e in range(count):
                    for i, entries in enumerate((gt_sb, gs_sb)):
                        looked_up = gists[first + e][:].indirect(entries[:, ls])
                        if on_vector:
                            nc.vector.tensor_copy(out=fetched[i][:, e, :], in_=looked_up)
                        else:
                            nc.scalar.activation(out=fetched[i][:, e, :], in_=looked_up, func=ACT.Copy)
                nc.vector.scalar_tensor_tensor(
                    out=zd[:], in0=fetched[1][:], scalar=-0.6, in1=fetched[0][:], op0=ALU.mult, op1=ALU.add
                )
            gated = ring.tile([P, count, width], F32, name="gated")
            gate = gates[first // 2][:, first % 2 : first % 2 + count, rs]
            nc.vector.scalar_tensor_tensor(out=gated[:], in0=gate, scalar=1.0, in1=zd[:], op0=ALU.add, op1=ALU.mult)
            for e in range(count):
                t = first + e
                nc.vector.scalar_tensor_tensor(
                    out=hid_planes[:, t, rs],
                    in0=loc_sb[:, t, rs],
                    scalar=part_unit[:, t : t + 1],
                    in1=gated[:, e, :],
                    op0=ALU.mult,
                    op1=ALU.add,
                )

        def finish(start, width):
            rs = slice(start, start + width)
            hid = keep.tile([P, width, PACK], BF16, name="hid%d" % start, align_bytes=64)
            weave = nc.vector.tensor_copy if start + width == U else nc.scalar.copy
            weave(
                out=hid[:].rearrange("p (c i) t -> p c t i", i=4),
                in_=hid_planes[:, :, rs].rearrange("p t (c i) -> p c t i", i=4),
            )
            h_codes = keep.tile([P, width], U32, name="h_codes%d" % start, align_bytes=64)
            h_plane = keep.tile([P, width], U8, name="h_plane%d" % start, align_bytes=64)
            nc.vector.quantize_mx(out=h_codes[:].bitcast(FP8X4), scales=h_plane[:], in_=hid[:].rearrange("p r t -> p (r t)"))
            res = value_banks.tile([P, width], F32, name="bank")
            nc.tensor.matmul_mx(
                out=res[:],
                lhsT=w3_codes[:].bitcast(FP4X4),
                lhsT_scale=w3_plane[:],
                rhs=h_codes[:].bitcast(FP8X4),
                rhs_scale=h_plane[:],
                start=True,
                stop=True,
            )
            res_sb = keep.tile([P, width], F32, name="res_sb%d" % start)
            nc.scalar.copy(out=res_sb[:], in_=res[:])
            nc.sync.dma_start(out=out[:, rs], in_=res_sb[:])

        last = len(UNITS) - 1
        for u in range(len(UNITS)):
            products(u)
            if FIRST_GATE <= u < FIRST_GATE + PACK:
                make_gate(u)
            if u > 0:
                add_weights(u - 1)
        add_weights(last)
        average_first()
        invs = keep.tile([P, PACK - 1, BLOCKS, P], F32, name="invs", tag="th%d" % last)
        for t in range(1, PACK):
            average_late(t, invs[:, t - 1])
        read(0, 1, 0, U // 2, 2)
        read(0, 1, U // 2, U // 2, 1)
        read(1, 1, 0, U, 1)
        for start, width in CHUNKS:
            read(2, 2, start, width, 0)
            finish(start, width)
